import numpy as np
import ml_dtypes


def mxq(x, axis, fmt="e4m3"):
    dtype, down = {"e4m3": (ml_dtypes.float8_e4m3fn, 7), "e5m2": (ml_dtypes.float8_e5m2, 14)}[fmt]
    v = np.moveaxis(np.asarray(x, np.float32).astype(ml_dtypes.bfloat16).astype(np.float64), axis, -1)
    blocks = v.reshape(v.shape[:-1] + (-1, 32))
    amax = np.abs(blocks).max(-1, keepdims=True)
    byte = np.maximum(np.where(amax > 0, np.frexp(amax)[1] - 1 + 127, 0) - down, 1)
    scale = np.exp2(byte - 127.0)
    codes = (blocks / scale).astype(np.float32).astype(dtype).astype(np.float64)
    return np.moveaxis((codes * scale).reshape(v.shape), -1, axis)


WIDE = False


def mx_kscale(k):
    if not WIDE:
        return np.ones(k)
    levels = np.array([10, -10, 5, -5, 0])
    if k % 512:
        return np.exp2(np.random.permutation(np.resize(levels, k // 32))).repeat(32)
    a = np.empty((k // 512, 16))
    for p in range(k // 512):
        a[p, :8] = np.random.permutation(np.resize(levels, 8))
        for g in range(8):
            far = levels[np.abs(levels - a[p, g]) >= 10]
            a[p, g + 8] = far[np.random.randint(len(far))]
    return np.exp2(a.ravel()).repeat(32)


BF16 = ml_dtypes.bfloat16


def bf(x):
    return np.asarray(x, np.float32).astype(BF16)


def f64(x):
    return np.asarray(x).astype(np.float64)


E2M1 = np.array([0.0, 0.5, 1.0, 1.5, 2.0, 3.0, 4.0, 6.0, -0.0, -0.5, -1.0, -1.5, -2.0, -3.0, -4.0, -6.0])


def pack_weight(w, fmt):
    k, n = w.shape
    w = f64(bf(w)).reshape(k // 32, 32, n)
    amax = np.abs(w).max(1)
    if fmt == "e4m3":
        byte = np.frexp(amax)[1] - 1 + 127 - 7
    else:
        mant, ex = np.frexp(amax / 6.0)
        byte = np.where(mant > 0.5, ex, ex - 1) + 127
    byte = np.clip(np.where(amax > 0, byte, 1), 1, 254)
    scaled = (w * np.exp2(127.0 - byte)[:, None, :]).reshape(k, n).astype(np.float32)
    by_word = np.ascontiguousarray(scaled.reshape(k // 512, 128, 4, n).transpose(0, 1, 3, 2))
    if fmt == "e4m3":
        words = by_word.astype(ml_dtypes.float8_e4m3fn).view(np.uint8)
    else:
        c = by_word.astype(ml_dtypes.float4_e2m1fn).view(np.uint8) & 0xF
        words = c[..., 0::2] | (c[..., 1::2] << 4)
    return np.ascontiguousarray(words), np.ascontiguousarray(byte.astype(np.uint8).reshape(k // 512, 16, n))


def unpack_weight(words, scales, fmt):
    g, p, n, _ = words.shape
    if fmt == "e4m3":
        vals = np.ascontiguousarray(words).view(ml_dtypes.float8_e4m3fn).astype(np.float64)
    else:
        nib = np.empty((g, p, n, 4), np.uint8)
        nib[..., 0::2] = words & 0xF
        nib[..., 1::2] = words >> 4
        vals = E2M1[nib]
    vals = vals * np.repeat(np.exp2(scales.astype(np.float64) - 127.0), 8, axis=1)[..., None]
    return vals.transpose(0, 1, 3, 2).reshape(g * 512, n)
def pack4(w):
    words, scales = pack_weight(w, "e2m1")
    return words.reshape(words.shape[0], 128, -1), scales


def unpack4(words, scales):
    return unpack_weight(words.reshape(words.shape[0], 128, -1, 2), scales, "e2m1")


A, K, D = 1024, 512, 1536


def draw0():
    s, t = mx_kscale(K), mx_kscale(A)
    code = np.random.standard_normal((A, K)) * s * t[:, None]
    dictionary = np.random.standard_normal((K, D)) / np.sqrt(K) / s[:, None]
    prev = np.random.standard_normal((A, D)) * t[:, None]
    gstep = 0.5 * np.random.standard_normal((A, D))
    mix = np.eye(A) + np.random.standard_normal((A, A)) / np.sqrt(A)
    avg = 0.5 * (np.eye(A) + np.random.standard_normal((A, A)) / np.sqrt(A))
    mix_words, mix_scales = pack4(mix / t[:, None])
    avg_words, avg_scales = pack4(avg / t[:, None])
    return {"code": bf(code), "dictionary": bf(dictionary),
            "prev": bf(prev), "gstep": bf(gstep),
            "mix_words": mix_words, "mix_scales": mix_scales,
            "avg_words": avg_words, "avg_scales": avg_scales}


def core(code, dictionary, prev, gstep, mix_words, mix_scales, avg_words, avg_scales):
    x0 = f64(prev)
    mix = unpack4(mix_words, mix_scales)
    avg = unpack4(avg_words, avg_scales)
    x1 = (mxq(f64(code), 1, "e4m3") @ mxq(f64(dictionary), 0, "e4m3")) + x0
    now = mix.T @ mxq(x1, 0, "e4m3")
    before = avg.T @ mxq(x0, 0, "e4m3")
    return now - before - f64(gstep)


def e4m3fn_bytes(y):
    return np.clip(np.asarray(y, np.float64), -448.0, 448.0).astype(np.float32).astype(ml_dtypes.float8_e4m3fn).view(np.uint8)


def e4m3fn_values(b):
    return np.asarray(b, np.uint8).view(ml_dtypes.float8_e4m3fn).astype(np.float64)


def setup_inputs():
    d = draw0()
    x0 = np.asarray(d['dictionary']).astype(np.float64)
    s = (np.max(np.abs(x0), axis=(1,), keepdims=True) / 448.0).astype(np.float32)
    out = {}
    for k, v in d.items():
        if k == 'dictionary':
            out['dictionary_bytes'] = e4m3fn_bytes(x0 / s.astype(np.float64))
            out['dictionary_scale'] = s
        else:
            out[k] = v
    return out


def reference(code, dictionary_bytes, dictionary_scale, prev, gstep, mix_words, mix_scales, avg_words, avg_scales):
    return core(code, e4m3fn_values(dictionary_bytes) * dictionary_scale.astype(np.float64), prev, gstep, mix_words, mix_scales, avg_words, avg_scales)

@@ -1,0 +1,315 @@
+from contextlib import ExitStack
+
+import concourse.mybir as mybir
+from concourse.masks import make_identity
+
+A, K, D = 1024, 512, 1536
+FLOPS = 2 * A * K * D + 2 * (2 * A * A * D)
+
+F32 = mybir.dt.float32
+BF16 = mybir.dt.bfloat16
+I32 = mybir.dt.int32
+U32 = mybir.dt.uint32
+U8 = mybir.dt.uint8
+FP8 = mybir.dt.float8_e4m3fn
+FP8X4 = mybir.dt.float8_e4m3fn_x4
+FP4X4 = mybir.dt.float4_e2m1fn_x4
+ALU = mybir.AluOpType
+COPY = mybir.ActivationFunctionType.Copy
+
+P = 128
+T = 4
+G = A // 512
+C = 3
+W = D // C
+B = W // P
+M = A // P
+UNITS = G * B
+AHEAD = 4
+GP_SUB = ()
+GP_NEG = ((0, 1),)
+
+
+def tile_extra_consensus_step_s13_kernel(
+    tc, code, dictionary_bytes, dictionary_scale, prev, gstep, mix_words, mix_scales, avg_words, avg_scales, out
+):
+    nc = tc.nc
+    with ExitStack() as ctx:
+        keep = ctx.enter_context(tc.tile_pool(name="keep", bufs=1))
+        flow = ctx.enter_context(tc.tile_pool(name="flow", bufs=8))
+        psum = ctx.enter_context(tc.psum_pool(name="psum", bufs=1))
+
+        def sb(name, shape, dtype):
+            return keep.tile(shape, dtype, name=name, align_bytes=64)
+
+        ident = sb("ident", [P, P], F32)
+        make_identity(nc, ident[:])
+        planes = sb("planes", [P, 2 * G, A], U8)
+        warm_in = sb("warm_in", [P, 16], F32)
+        warm_out = sb("warm_out", [P, 16], F32)
+
+        ctx.enter_context(tc.manual_schedule())
+
+        dscale = sb("dscale", [P, T], F32)
+        dbytes = [sb("dbytes0", [P, T, W], U8), sb("dbytes12", [P, T, 2 * W], U8)]
+        code_sb = [sb(f"code{g}", [P, T, K], BF16) for g in range(G)]
+        prev_sb = [[sb(f"prev{g}_{c}", [P, T, W], BF16) for c in range(C)] for g in range(G)]
+        words = [sb("avg_w", [P, G, 2 * A], U8), sb("mix_w", [P, G, 2 * A], U8)]
+        gst = [sb(f"gstep{i}", [P, 2, D], BF16) for i in range(M // 2)]
+
+        nc.gpsimd.memset(planes[:].bitcast(I32), 0)
+        nc.vector.memset(warm_in[:], 0.0)
+        nc.scalar.activation(out=warm_out[:], in_=warm_in[:], func=COPY, scale=-1.0)
+
+        load = nc.sync.dma_start
+        dict_v = dictionary_bytes.rearrange("(p t) n -> p t n", t=T)
+        code_v = code.rearrange("(g m t) k -> g m t k", m=P, t=T)
+        prev_v = prev.rearrange("(g p t) d -> g p t d", p=P, t=T)
+        gstep_v = gstep.rearrange("(m p) d -> p m d", p=P)
+
+        def load_prev(c, g):
+            load(out=prev_sb[g][c][:], in_=prev_v[g][:, :, c * W : (c + 1) * W])
+
+        def load_gstep(i):
+            load(out=gst[i][:], in_=gstep_v[:, 2 * i : 2 * i + 2, :])
+
+        def load_mixer(which, w_hbm, s_hbm):
+            load(out=words[which][:].bitcast(I32), in_=w_hbm.rearrange("g p b -> p g b").bitcast(I32))
+            rows = s_hbm.bitcast(I32).rearrange("g (q i) n -> i q g n", i=4)
+            for i in range(4):
+                load(out=planes[i:P:32, G * which : G * which + G, :].bitcast(I32), in_=rows[i])
+
+        load(out=dscale[:], in_=dictionary_scale.rearrange("(p t) o -> p (t o)", t=T))
+        load(out=dbytes[0][:], in_=dict_v[:, :, 0:W])
+        load(out=code_sb[0][:], in_=code_v[0])
+        load_prev(0, 0)
+        load(out=code_sb[1][:], in_=code_v[1])
+        load_prev(0, 1)
+        load_mixer(0, avg_words, avg_scales)
+        load_mixer(1, mix_words, mix_scales)
+        load(out=dbytes[1][:], in_=dict_v[:, :, W:D])
+        load_prev(1, 0)
+        load_prev(1, 1)
+        load_gstep(0)
+        load_gstep(1)
+        load_prev(2, 0)
+        load_prev(2, 1)
+        load_gstep(2)
+        load_gstep(3)
+
+        code_grp = [sb(f"code_grp{g}", [P, T, P, T], BF16) for g in range(G)]
+        code_q = [sb(f"code_q{g}", [P, T * P], U32) for g in range(G)]
+        code_s = [sb(f"code_s{g}", [P, T * P], U8) for g in range(G)]
+        turned = {}
+
+        def turn(g, h):
+            bank = psum.tile([P, 2, 2, P], F32, name="turn", tag="late", bufs=5)
+            for j in range(2):
+                w = code_sb[g][:, 2 * h + j, :].bitcast(F32)
+                for u in range(2):
+                    nc.tensor.transpose(bank[:, j, u, :], w[:, u : K // 2 : 2], ident[:])
+            turned[g, h] = bank
+
+        def untangle(copy, g, h):
+            copy(
+                out=code_grp[g][:, 2 * h : 2 * h + 2].rearrange("p j m t -> p j (m t)").bitcast(F32).rearrange("p j (m u) -> p j m u", u=2),
+                in_=turned[g, h][:].rearrange("p j u m -> p j m u"),
+            )
+
+        def quant(src, codes, scales):
+            nc.vector.quantize_mx(out=codes[:].bitcast(FP8X4), scales=scales[:], in_=src)
+
+        def quant_code(g):
+            quant(code_grp[g][:].rearrange("p a m t -> p (a m t)"), code_q[g], code_s[g])
+
+        dwide = [sb(f"dwide{c}", [P, T, W], BF16) for c in range(C)]
+        dgrp = [sb(f"dgrp{c}", [P, W, T], BF16) for c in range(C)]
+        dict_q = [sb(f"dict_q{c}", [P, W], U32) for c in range(C)]
+        dict_s = [sb(f"dict_s{c}", [P, W], U8) for c in range(C)]
+
+        def widen(c, t):
+            src = dbytes[0][:, t, :] if c == 0 else dbytes[1][:, t, (c - 1) * W : c * W]
+            src = src.bitcast(FP8)
+            if c == 0:
+                nc.vector.tensor_scalar(out=dwide[c][:, t, :], in0=src, scalar1=dscale[:, t : t + 1], scalar2=None, op0=ALU.mult)
+            else:
+                nc.scalar.activation(out=dwide[c][:, t, :], in_=src, func=COPY, scale=dscale[:, t : t + 1])
+
+        def group_dict(copy, c, lo, hi):
+            copy(out=dgrp[c][:, lo:hi, :], in_=dwide[c][:, :, lo:hi].rearrange("p t n -> p n t"))
+
+        def quant_dict(c):
+            quant(dgrp[c][:].rearrange("p n t -> p (n t)"), dict_q[c], dict_s[c])
+
+        neg = [[sb(f"neg{g}_{c}", [P, W, T], BF16) for c in range(C)] for g in range(G)]
+        neg_q = [[sb(f"neg_q{g}_{c}", [P, W], U32) for c in range(C)] for g in range(G)]
+        neg_s = [[sb(f"neg_s{g}_{c}", [P, W], U8) for c in range(C)] for g in range(G)]
+
+        def negate(c, g, lo, hi):
+            src = prev_sb[g][c][:, :, lo:hi].rearrange("p t n -> p n t")
+            dst = neg[g][c][:, lo:hi, :]
+            if (c, g) in GP_NEG:
+                nc.gpsimd.tensor_scalar(out=dst, in0=src, scalar1=-1.0, scalar2=0.0, op0=ALU.mult, op1=ALU.add)
+            else:
+                nc.scalar.activation(out=dst, in_=src, func=COPY, scale=-1.0)
+
+        def quant_neg(c, g):
+            quant(neg[g][c][:].rearrange("p n t -> p (n t)"), neg_q[g][c], neg_s[g][c])
+
+        x1_q = [[sb(f"x1_q{g}_{c}", [P, W], U32) for c in range(C)] for g in range(G)]
+        x1_s = [[sb(f"x1_s{g}_{c}", [P, W], U8) for c in range(C)] for g in range(G)]
+        x1_grp = {}
+        first = {}
+
+        def stage1(c, u):
+            g, b = divmod(u, B)
+            cols = slice(b * P, (b + 1) * P)
+            bank = psum.tile([P, T, P], F32, name="first", tag="first", bufs=3)
+            for t in range(T):
+                rows = slice(t * P, (t + 1) * P)
+                nc.tensor.matmul_mx(
+                    out=bank[:, t, :],
+                    lhsT=code_q[g][:, rows].bitcast(FP8X4),
+                    lhsT_scale=code_s[g][:, rows],
+                    rhs=dict_q[c][:, cols].bitcast(FP8X4),
+                    rhs_scale=dict_s[c][:, cols],
+                    start=True,
+                    stop=True,
+                )
+            first[c, u] = bank
+
+        def add_prev(c, u):
+            g, b = divmod(u, B)
+            if b == 0:
+                x1_grp[c, g] = flow.tile([P, W, T], BF16, name="x1_grp", bufs=3, align_bytes=64)
+            cols = slice(b * P, (b + 1) * P)
+            nc.vector.tensor_tensor(
+                out=x1_grp[c, g][:, cols, :],
+                in0=first[c, u][:].rearrange("p t n -> p n t"),
+                in1=neg[g][c][:, cols, :],
+                op=ALU.subtract,
+            )
+
+        def quant_x1(c, g):
+            quant(x1_grp[c, g][:].rearrange("p n t -> p (n t)"), x1_q[g][c], x1_s[g][c])
+
+        late = {}
+
+        def mix_pass(j, which, g, codes, scales, start, stop):
+            c, m = divmod(j, M)
+            nc.tensor.matmul_mx(
+                out=late[j][:],
+                lhsT=words[which][:, g, 2 * P * m : 2 * P * (m + 1)].bitcast(FP4X4),
+                lhsT_scale=planes[:, G * which + g, P * m : P * (m + 1)],
+                rhs=codes[g][c][:].bitcast(FP8X4),
+                rhs_scale=scales[g][c][:],
+                start=start,
+                stop=stop,
+            )
+
+        def average(j):
+            if j < C * M:
+                late[j] = psum.tile([P, W], F32, name="late", tag="late", bufs=5)
+                for g in range(G):
+                    mix_pass(j, 0, g, neg_q, neg_s, g == 0, False)
+
+        def mix(j):
+            for g in range(G):
+                mix_pass(j, 1, g, x1_q, x1_s, False, g == G - 1)
+
+        def finish(j):
+            c, m = divmod(j, M)
+            cols = slice(c * W, (c + 1) * W)
+            res = flow.tile([P, W], F32, name="res", bufs=8, align_bytes=64)
+            step = gst[m // 2][:, m % 2, cols]
+            if j in GP_SUB:
+                raw = flow.tile([P, W], F32, name="raw", bufs=3, align_bytes=64)
+                nc.scalar.copy(out=raw[:], in_=late[j][:])
+                nc.gpsimd.tensor_tensor(out=res[:], in0=raw[:], in1=step, op=ALU.subtract)
+            else:
+                nc.vector.tensor_tensor(out=res[:], in0=late[j][:], in1=step, op=ALU.subtract)
+            nc.sync.dma_start(out=out[m * P : (m + 1) * P, cols], in_=res[:])
+
+        vcopy, scopy = nc.vector.tensor_copy, nc.scalar.copy
+        for t in range(T):
+            widen(0, t)
+        group_dict(vcopy, 0, 0, W)
+        turn(0, 0)
+        turn(0, 1)
+        untangle(scopy, 0, 0)
+        untangle(scopy, 0, 1)
+        quant_dict(0)
+        quant_code(0)
+        turn(1, 0)
+        turn(1, 1)
+        negate(0, 0, 0, P)
+        negate(0, 0, P, 2 * P)
+        untangle(scopy, 1, 0)
+        untangle(vcopy, 1, 1)
+        negate(0, 0, 2 * P, 3 * P)
+        negate(0, 0, 3 * P, 4 * P)
+        for b in range(B):
+            negate(0, 1, b * P, (b + 1) * P)
+        for t in range(T):
+            widen(1, t)
+        group_dict(scopy, 1, 0, W // 2)
+        group_dict(scopy, 1, W // 2, W)
+        for h in range(2):
+            negate(1, 0, h * W // 2, (h + 1) * W // 2)
+
+        stage1(0, 0)
+        stage1(0, 1)
+        for u in range(UNITS):
+            if u == 2:
+                quant_code(1)
+            if u + 2 < UNITS:
+                stage1(0, u + 2)
+            add_prev(0, u)
+            if u == 3:
+                quant_neg(0, 0)
+            if u == 4:
+                quant_x1(0, 0)
+            if u == 6:
+                quant_neg(0, 1)
+                average(0)
+                average(1)
+        quant_dict(1)
+        quant_x1(0, 1)
+        average(2)
+        average(3)
+
+        for c in range(C):
+            more = c + 1 < C
+            if more:
+                stage1(c + 1, 0)
+                stage1(c + 1, 1)
+            for i in range(M):
+                j = c * M + i
+                if more:
+                    if i < 2:
+                        negate(c + 1, 1, i * W // 2, (i + 1) * W // 2)
+                    elif c + 2 < C:
+                        if i < 4:
+                            widen(c + 2, 2 * (i - 2))
+                            widen(c + 2, 2 * (i - 2) + 1)
+                        elif i < 6:
+                            group_dict(scopy, c + 2, (i - 4) * W // 2, (i - 3) * W // 2)
+                        else:
+                            negate(c + 2, 0, (i - 6) * W // 2, (i - 5) * W // 2)
+                mix(j)
+                if more:
+                    if i + 2 < UNITS:
+                        stage1(c + 1, i + 2)
+                    add_prev(c + 1, i)
+                    if i == 1:
+                        quant_neg(c + 1, 0)
+                    if i == 2:
+                        quant_neg(c + 1, 1)
+                    if i == 4:
+                        quant_x1(c + 1, 0)
+                average(j + AHEAD)
+                finish(j)
+                if c + 2 < C and i == 6:
+                    quant_dict(c + 2)
+            if more:
+                quant_x1(c + 1, 1)

@@ -20,14 +20,17 @@ COPY = mybir.ActivationFunctionType.Copy
 P = 128
 T = 4
 G = A // 512
-C = 3
-W = D // C
-B = W // P
 M = A // P
-UNITS = G * B
+WIDTHS = (512, 512, 512)
+STARTS = tuple(sum(WIDTHS[:c]) for c in range(len(WIDTHS)))
+C = len(WIDTHS)
+PIECES = ((0,), (1,), (2,))
 AHEAD = 4
-GP_SUB = ()
-GP_NEG = ((0, 1),)
+LATE = 5
+EARLY = 8 - LATE
+GP_SUB = (2,4,6,8)
+V_WIDEN = (0,)
+GROUPERS = ("v", "s", "s")
 
 
 def tile_extra_consensus_step_s13_kernel(
@@ -51,9 +54,16 @@ def tile_extra_consensus_step_s13_kernel(
         ctx.enter_context(tc.manual_schedule())
 
         dscale = sb("dscale", [P, T], F32)
-        dbytes = [sb("dbytes0", [P, T, W], U8), sb("dbytes12", [P, T, 2 * W], U8)]
         code_sb = [sb(f"code{g}", [P, T, K], BF16) for g in range(G)]
-        prev_sb = [[sb(f"prev{g}_{c}", [P, T, W], BF16) for c in range(C)] for g in range(G)]
+        dbytes, prev_sb = {}, {}
+        piece_cols = []
+        for i, chunks in enumerate(PIECES):
+            lo = STARTS[chunks[0]]
+            hi = STARTS[chunks[-1]] + WIDTHS[chunks[-1]]
+            piece_cols.append((lo, hi))
+            dbytes[i] = sb(f"dbytes{i}", [P, T, hi - lo], U8)
+            for g in range(G):
+                prev_sb[i, g] = sb(f"prev{i}_{g}", [P, T, hi - lo], BF16)
         words = [sb("avg_w", [P, G, 2 * A], U8), sb("mix_w", [P, G, 2 * A], U8)]
         gst = [sb(f"gstep{i}", [P, 2, D], BF16) for i in range(M // 2)]
 
@@ -67,35 +77,49 @@ def tile_extra_consensus_step_s13_kernel(
         prev_v = prev.rearrange("(g p t) d -> g p t d", p=P, t=T)
         gstep_v = gstep.rearrange("(m p) d -> p m d", p=P)
 
-        def load_prev(c, g):
-            load(out=prev_sb[g][c][:], in_=prev_v[g][:, :, c * W : (c + 1) * W])
+        def load_code(g, lo=0, hi=T):
+            load(out=code_sb[g][:, lo:hi], in_=code_v[g][:, lo:hi])
+
+        def load_prev(i, g):
+            lo, hi = piece_cols[i]
+            load(out=prev_sb[i, g][:], in_=prev_v[g][:, :, lo:hi])
+
+        def load_dict(i):
+            lo, hi = piece_cols[i]
+            load(out=dbytes[i][:], in_=dict_v[:, :, lo:hi])
 
         def load_gstep(i):
             load(out=gst[i][:], in_=gstep_v[:, 2 * i : 2 * i + 2, :])
 
-        def load_mixer(which, w_hbm, s_hbm):
-            load(out=words[which][:].bitcast(I32), in_=w_hbm.rearrange("g p b -> p g b").bitcast(I32))
+        def load_scales(which, s_hbm):
             rows = s_hbm.bitcast(I32).rearrange("g (q i) n -> i q g n", i=4)
             for i in range(4):
                 load(out=planes[i:P:32, G * which : G * which + G, :].bitcast(I32), in_=rows[i])
 
+        def load_words(which, w_hbm):
+            load(out=words[which][:].bitcast(I32), in_=w_hbm.rearrange("g p b -> p g b").bitcast(I32))
+
         load(out=dscale[:], in_=dictionary_scale.rearrange("(p t) o -> p (t o)", t=T))
-        load(out=dbytes[0][:], in_=dict_v[:, :, 0:W])
-        load(out=code_sb[0][:], in_=code_v[0])
+        load_dict(0)
+        load_code(0, 0, 2)
+        load_code(0, 2, 4)
         load_prev(0, 0)
-        load(out=code_sb[1][:], in_=code_v[1])
+        load_code(1)
         load_prev(0, 1)
-        load_mixer(0, avg_words, avg_scales)
-        load_mixer(1, mix_words, mix_scales)
-        load(out=dbytes[1][:], in_=dict_v[:, :, W:D])
+        load_dict(1)
+        load_words(0, avg_words)
+        load_scales(0, avg_scales)
+        load_scales(1, mix_scales)
         load_prev(1, 0)
+        load_words(1, mix_words)
         load_prev(1, 1)
         load_gstep(0)
+        load_dict(2)
         load_gstep(1)
-        load_prev(2, 0)
-        load_prev(2, 1)
         load_gstep(2)
+        load_prev(2, 0)
         load_gstep(3)
+        load_prev(2, 1)
 
         code_grp = [sb(f"code_grp{g}", [P, T, P, T], BF16) for g in range(G)]
         code_q = [sb(f"code_q{g}", [P, T * P], U32) for g in range(G)]
@@ -103,7 +127,7 @@ def tile_extra_consensus_step_s13_kernel(
         turned = {}
 
         def turn(g, h):
-            bank = psum.tile([P, 2, 2, P], F32, name="turn", tag="late", bufs=5)
+            bank = psum.tile([P, 2, 2, P], F32, name="turn", tag="late", bufs=LATE)
             for j in range(2):
                 w = code_sb[g][:, 2 * h + j, :].bitcast(F32)
                 for u in range(2):
@@ -111,60 +135,80 @@ def tile_extra_consensus_step_s13_kernel(
             turned[g, h] = bank
 
         def untangle(copy, g, h):
+            dst = code_grp[g][:, 2 * h : 2 * h + 2].rearrange("p j m t -> p j (m t)").bitcast(F32)
             copy(
-                out=code_grp[g][:, 2 * h : 2 * h + 2].rearrange("p j m t -> p j (m t)").bitcast(F32).rearrange("p j (m u) -> p j m u", u=2),
+                out=dst.rearrange("p j (m u) -> p j m u", u=2),
                 in_=turned[g, h][:].rearrange("p j u m -> p j m u"),
             )
 
         def quant(src, codes, scales):
-            nc.vector.quantize_mx(out=codes[:].bitcast(FP8X4), scales=scales[:], in_=src)
+            nc.vector.quantize_mx(out=codes.bitcast(FP8X4), scales=scales, in_=src)
 
         def quant_code(g):
-            quant(code_grp[g][:].rearrange("p a m t -> p (a m t)"), code_q[g], code_s[g])
+            quant(code_grp[g][:].rearrange("p a m t -> p (a m t)"), code_q[g][:], code_s[g][:])
 
-        dwide = [sb(f"dwide{c}", [P, T, W], BF16) for c in range(C)]
-        dgrp = [sb(f"dgrp{c}", [P, W, T], BF16) for c in range(C)]
-        dict_q = [sb(f"dict_q{c}", [P, W], U32) for c in range(C)]
-        dict_s = [sb(f"dict_s{c}", [P, W], U8) for c in range(C)]
+        piece_of = {}
+        for i, chunks in enumerate(PIECES):
+            for c in chunks:
+                piece_of[c] = i, STARTS[c] - piece_cols[i][0]
 
-        def widen(c, t):
-            src = dbytes[0][:, t, :] if c == 0 else dbytes[1][:, t, (c - 1) * W : c * W]
-            src = src.bitcast(FP8)
-            if c == 0:
-                nc.vector.tensor_scalar(out=dwide[c][:, t, :], in0=src, scalar1=dscale[:, t : t + 1], scalar2=None, op0=ALU.mult)
+        dwide = [sb(f"dwide{c}", [P, T, WIDTHS[c]], BF16) for c in range(C)]
+        dgrp = [sb(f"dgrp{c}", [P, WIDTHS[c], T], BF16) for c in range(C)]
+        dict_q = [sb(f"dict_q{c}", [P, WIDTHS[c]], U32) for c in range(C)]
+        dict_s = [sb(f"dict_s{c}", [P, WIDTHS[c]], U8) for c in range(C)]
+
+        def widen(on, c, t, lo, hi):
+            src = dbytes[c][:, t, lo:hi].bitcast(FP8)
+            dst = dwide[c][:, t, lo:hi]
+            factor = dscale[:, t : t + 1]
+            if on == "v":
+                nc.vector.tensor_scalar(out=dst, in0=src, scalar1=factor, scalar2=None, op0=ALU.mult)
             else:
-                nc.scalar.activation(out=dwide[c][:, t, :], in_=src, func=COPY, scale=dscale[:, t : t + 1])
+                nc.scalar.activation(out=dst, in_=src, func=COPY, scale=factor)
 
-        def group_dict(copy, c, lo, hi):
-            copy(out=dgrp[c][:, lo:hi, :], in_=dwide[c][:, :, lo:hi].rearrange("p t n -> p n t"))
+        def group_dict(c, lo, hi):
+            src = dwide[c][:, :, lo:hi].rearrange("p t n -> p n t")
+            dst = dgrp[c][:, lo:hi, :]
+            if GROUPERS[c] == "v":
+                nc.vector.tensor_copy(out=dst, in_=src)
+            elif GROUPERS[c] == "s":
+                nc.scalar.copy(out=dst, in_=src)
+            else:
+                nc.gpsimd.tensor_scalar(out=dst, in0=src, scalar1=1.0, scalar2=0.0, op0=ALU.mult, op1=ALU.add)
 
         def quant_dict(c):
-            quant(dgrp[c][:].rearrange("p n t -> p (n t)"), dict_q[c], dict_s[c])
+            quant(dgrp[c][:].rearrange("p n t -> p (n t)"), dict_q[c][:], dict_s[c][:])
 
-        neg = [[sb(f"neg{g}_{c}", [P, W, T], BF16) for c in range(C)] for g in range(G)]
-        neg_q = [[sb(f"neg_q{g}_{c}", [P, W], U32) for c in range(C)] for g in range(G)]
-        neg_s = [[sb(f"neg_s{g}_{c}", [P, W], U8) for c in range(C)] for g in range(G)]
+        neg = {(c, g): sb(f"neg{c}_{g}", [P, WIDTHS[c], T], BF16) for c in range(C) for g in range(G)}
+        neg_q = {(c, g): sb(f"neg_q{c}_{g}", [P, WIDTHS[c]], U32) for c in range(C) for g in range(G)}
+        neg_s = {(c, g): sb(f"neg_s{c}_{g}", [P, WIDTHS[c]], U8) for c in range(C) for g in range(G)}
 
-        def negate(c, g, lo, hi):
-            src = prev_sb[g][c][:, :, lo:hi].rearrange("p t n -> p n t")
-            dst = neg[g][c][:, lo:hi, :]
-            if (c, g) in GP_NEG:
+        def negate(on, c, g, lo, hi):
+            i, at = piece_of[c]
+            src = prev_sb[i, g][:, :, at + lo : at + hi].rearrange("p t n -> p n t")
+            dst = neg[c, g][:, lo:hi, :]
+            if on == "g":
                 nc.gpsimd.tensor_scalar(out=dst, in0=src, scalar1=-1.0, scalar2=0.0, op0=ALU.mult, op1=ALU.add)
             else:
                 nc.scalar.activation(out=dst, in_=src, func=COPY, scale=-1.0)
 
         def quant_neg(c, g):
-            quant(neg[g][c][:].rearrange("p n t -> p (n t)"), neg_q[g][c], neg_s[g][c])
+            quant(neg[c, g][:].rearrange("p n t -> p (n t)"), neg_q[c, g][:], neg_s[c, g][:])
 
-        x1_q = [[sb(f"x1_q{g}_{c}", [P, W], U32) for c in range(C)] for g in range(G)]
-        x1_s = [[sb(f"x1_s{g}_{c}", [P, W], U8) for c in range(C)] for g in range(G)]
+        x1_q = {(c, g): sb(f"x1_q{c}_{g}", [P, WIDTHS[c]], U32) for c in range(C) for g in range(G)}
+        x1_s = {(c, g): sb(f"x1_s{c}_{g}", [P, WIDTHS[c]], U8) for c in range(C) for g in range(G)}
         x1_grp = {}
         first = {}
 
+        def units(c):
+            return G * WIDTHS[c] // P
+
         def stage1(c, u):
-            g, b = divmod(u, B)
+            if u >= units(c):
+                return
+            g, b = divmod(u, WIDTHS[c] // P)
             cols = slice(b * P, (b + 1) * P)
-            bank = psum.tile([P, T, P], F32, name="first", tag="first", bufs=3)
+            bank = psum.tile([P, T, P], F32, name="first", tag="first", bufs=EARLY)
             for t in range(T):
                 rows = slice(t * P, (t + 1) * P)
                 nc.tensor.matmul_mx(
@@ -179,51 +223,65 @@ def tile_extra_consensus_step_s13_kernel(
             first[c, u] = bank
 
         def add_prev(c, u):
-            g, b = divmod(u, B)
+            g, b = divmod(u, WIDTHS[c] // P)
             if b == 0:
-                x1_grp[c, g] = flow.tile([P, W, T], BF16, name="x1_grp", bufs=3, align_bytes=64)
+                x1_grp[c, g] = flow.tile([P, WIDTHS[c], T], BF16, name="x1_grp", bufs=3, align_bytes=64)
             cols = slice(b * P, (b + 1) * P)
             nc.vector.tensor_tensor(
                 out=x1_grp[c, g][:, cols, :],
                 in0=first[c, u][:].rearrange("p t n -> p n t"),
-                in1=neg[g][c][:, cols, :],
+                in1=neg[c, g][:, cols, :],
                 op=ALU.subtract,
             )
 
         def quant_x1(c, g):
-            quant(x1_grp[c, g][:].rearrange("p n t -> p (n t)"), x1_q[g][c], x1_s[g][c])
+            quant(x1_grp[c, g][:].rearrange("p n t -> p (n t)"), x1_q[c, g][:], x1_s[c, g][:])
 
         late = {}
+        started = {}
 
-        def mix_pass(j, which, g, codes, scales, start, stop):
+        def mix_pass(j, b, k):
             c, m = divmod(j, M)
+            which, g = divmod(k, G)
+            wide = WIDTHS[c] == 512
+            cols = slice(0, 512) if wide else slice(b * P, (b + 1) * P)
+            codes, scales = ((neg_q, neg_s), (x1_q, x1_s))[which]
             nc.tensor.matmul_mx(
-                out=late[j][:],
+                out=late[j][:, cols],
                 lhsT=words[which][:, g, 2 * P * m : 2 * P * (m + 1)].bitcast(FP4X4),
                 lhsT_scale=planes[:, G * which + g, P * m : P * (m + 1)],
-                rhs=codes[g][c][:].bitcast(FP8X4),
-                rhs_scale=scales[g][c][:],
-                start=start,
-                stop=stop,
+                rhs=codes[c, g][:, cols].bitcast(FP8X4),
+                rhs_scale=scales[c, g][:, cols],
+                start=k == 0,
+                stop=k == 2 * G - 1,
             )
 
-        def average(j):
-            if j < C * M:
-                late[j] = psum.tile([P, W], F32, name="late", tag="late", bufs=5)
-                for g in range(G):
-                    mix_pass(j, 0, g, neg_q, neg_s, g == 0, False)
+        def advance(j, upto):
+            if j >= C * M:
+                return
+            if j not in late:
+                tag, bufs = ("late", LATE) if j < C * M - EARLY else ("first", EARLY)
+                late[j] = psum.tile([P, WIDTHS[j // M]], F32, name="late", tag=tag, bufs=bufs)
+                started[j] = 0
+            for k in range(started[j], upto):
+                mix_pass(j, 0, k)
+            started[j] = max(upto, started[j])
 
         def mix(j):
-            for g in range(G):
-                mix_pass(j, 1, g, x1_q, x1_s, False, g == G - 1)
+            advance(j, 2 * G)
+            if WIDTHS[j // M] < 512:
+                for b in range(1, WIDTHS[j // M] // P):
+                    for k in range(2 * G):
+                        mix_pass(j, b, k)
 
         def finish(j):
             c, m = divmod(j, M)
-            cols = slice(c * W, (c + 1) * W)
-            res = flow.tile([P, W], F32, name="res", bufs=8, align_bytes=64)
+            w = WIDTHS[c]
+            cols = slice(STARTS[c], STARTS[c] + w)
+            res = flow.tile([P, w], F32, name="res", bufs=12, align_bytes=64)
             step = gst[m // 2][:, m % 2, cols]
             if j in GP_SUB:
-                raw = flow.tile([P, W], F32, name="raw", bufs=3, align_bytes=64)
+                raw = flow.tile([P, w], F32, name="raw", bufs=3, align_bytes=64)
                 nc.scalar.copy(out=raw[:], in_=late[j][:])
                 nc.gpsimd.tensor_tensor(out=res[:], in0=raw[:], in1=step, op=ALU.subtract)
             else:
@@ -232,84 +290,103 @@ def tile_extra_consensus_step_s13_kernel(
 
         vcopy, scopy = nc.vector.tensor_copy, nc.scalar.copy
         for t in range(T):
-            widen(0, t)
-        group_dict(vcopy, 0, 0, W)
+            widen("v", 0, t, 0, 256)
+        for t in range(T):
+            widen("s", 0, t, 256, 512)
+        group_dict(0, 0, 256)
+        group_dict(0, 256, 512)
         turn(0, 0)
         turn(0, 1)
         untangle(scopy, 0, 0)
         untangle(scopy, 0, 1)
         quant_dict(0)
         quant_code(0)
-        turn(1, 0)
-        turn(1, 1)
-        negate(0, 0, 0, P)
-        negate(0, 0, P, 2 * P)
-        untangle(scopy, 1, 0)
-        untangle(vcopy, 1, 1)
-        negate(0, 0, 2 * P, 3 * P)
-        negate(0, 0, 3 * P, 4 * P)
-        for b in range(B):
-            negate(0, 1, b * P, (b + 1) * P)
-        for t in range(T):
-            widen(1, t)
-        group_dict(scopy, 1, 0, W // 2)
-        group_dict(scopy, 1, W // 2, W)
-        for h in range(2):
-            negate(1, 0, h * W // 2, (h + 1) * W // 2)
-
         stage1(0, 0)
         stage1(0, 1)
-        for u in range(UNITS):
-            if u == 2:
+        turn(1, 0)
+        turn(1, 1)
+        negate("s", 0, 0, 0, 128)
+        negate("s", 0, 0, 128, 256)
+        negate("g", 0, 0, 256, 384)
+        negate("g", 0, 0, 384, 512)
+        untangle(scopy, 1, 0)
+        untangle(scopy, 1, 1)
+        for b in range(4):
+            negate("g", 0, 1, b * 128, (b + 1) * 128)
+        for t in range(T):
+            widen("s", 1, t, 0, 512)
+        group_dict(1, 0, 256)
+        group_dict(1, 256, 512)
+        for b in range(4):
+            negate("g", 1, 0, b * 128, (b + 1) * 128)
+        for h in range(2):
+            negate("s", 1, 1, h * 256, (h + 1) * 256)
+
+        for u in range(8):
+            if u == 3:
                 quant_code(1)
-            if u + 2 < UNITS:
+                stage1(0, 4)
+            if u != 2:
                 stage1(0, u + 2)
             add_prev(0, u)
             if u == 3:
                 quant_neg(0, 0)
+                for j in range(LATE):
+                    advance(j, 1)
             if u == 4:
                 quant_x1(0, 0)
-            if u == 6:
+            if u == 5:
                 quant_neg(0, 1)
-                average(0)
-                average(1)
+                for j in range(LATE):
+                    advance(j, 2)
         quant_dict(1)
+        stage1(1, 0)
+        stage1(1, 1)
+        for j in range(LATE):
+            advance(j, 3)
         quant_x1(0, 1)
-        average(2)
-        average(3)
 
+        side = {
+            0: [lambda t=t: widen("s", 2, t, 0, 512) for t in range(T)]
+            + [lambda h=h: group_dict(2, h * 256, (h + 1) * 256) for h in range(2)]
+            + [lambda h=h: negate("s", 2, 0, h * 256, (h + 1) * 256) for h in range(2)],
+            1: [lambda h=h: negate("s", 2, 1, h * 256, (h + 1) * 256) for h in range(2)],
+        }
         for c in range(C):
             more = c + 1 < C
-            if more:
+            todo = side.get(c, [])
+            if c == 0:
+                mix(0)
+            if more and c > 0:
                 stage1(c + 1, 0)
                 stage1(c + 1, 1)
             for i in range(M):
                 j = c * M + i
+                for task in todo[:1]:
+                    task()
+                todo = todo[1:]
+                if j > 0:
+                    mix(j)
                 if more:
-                    if i < 2:
-                        negate(c + 1, 1, i * W // 2, (i + 1) * W // 2)
-                    elif c + 2 < C:
-                        if i < 4:
-                            widen(c + 2, 2 * (i - 2))
-                            widen(c + 2, 2 * (i - 2) + 1)
-                        elif i < 6:
-                            group_dict(scopy, c + 2, (i - 4) * W // 2, (i - 3) * W // 2)
-                        else:
-                            negate(c + 2, 0, (i - 6) * W // 2, (i - 5) * W // 2)
-                mix(j)
-                if more:
-                    if i + 2 < UNITS:
-                        stage1(c + 1, i + 2)
+                    stage1(c + 1, i + 2)
                     add_prev(c + 1, i)
                     if i == 1:
                         quant_neg(c + 1, 0)
-                    if i == 2:
+                    if i == 3:
                         quant_neg(c + 1, 1)
                     if i == 4:
                         quant_x1(c + 1, 0)
-                average(j + AHEAD)
+                if j + AHEAD < C * M - EARLY:
+                    advance(j + AHEAD, 2)
+                if c == C - 1 and i in (2, 4):
+                    advance(C * M - EARLY + i // 2, 3)
+                if more and i >= 5:
+                    advance((c + 1) * M + i - 5, 3)
                 finish(j)
                 if c + 2 < C and i == 6:
                     quant_dict(c + 2)
             if more:
                 quant_x1(c + 1, 1)
+            advance((c + 1) * M + 3, 3)
+            if c == C - 2:
+                advance(C * M - EARLY, 3)

@@ -28,6 +28,7 @@ PIECES = ((0,), (1,), (2,))
 AHEAD = 4
 LATE = 5
 EARLY = 8 - LATE
+DIRECT = ()
 GP_SUB = (2,4,6,8)
 V_WIDEN = (0,)
 GROUPERS = ("v", "s", "s")
@@ -67,8 +68,10 @@ def tile_extra_consensus_step_s13_kernel(
         words = [sb("avg_w", [P, G, 2 * A], U8), sb("mix_w", [P, G, 2 * A], U8)]
         gst = [sb(f"gstep{i}", [P, 2, D], BF16) for i in range(M // 2)]
 
-        nc.gpsimd.memset(planes[:].bitcast(I32), 0)
+        warm_w = sb("warm_w", [P, 512], BF16)
+        nc.vector.memset(warm_w[:], 0.0)
         nc.vector.memset(warm_in[:], 0.0)
+        nc.vector.memset(planes[:].bitcast(I32), 0)
         nc.scalar.activation(out=warm_out[:], in_=warm_in[:], func=COPY, scale=-1.0)
 
         load = nc.sync.dma_start
@@ -167,8 +170,8 @@ def tile_extra_consensus_step_s13_kernel(
                 nc.scalar.activation(out=dst, in_=src, func=COPY, scale=factor)
 
         def group_dict(c, lo, hi):
-            src = dwide[c][:, :, lo:hi].rearrange("p t n -> p n t")
-            dst = dgrp[c][:, lo:hi, :]
+            src = dwide[c][:, :, lo:hi].rearrange("p t (n i) -> p n t i", i=4)
+            dst = dgrp[c][:, lo:hi, :].rearrange("p (n i) t -> p n t i", i=4)
             if GROUPERS[c] == "v":
                 nc.vector.tensor_copy(out=dst, in_=src)
             elif GROUPERS[c] == "s":
@@ -185,8 +188,8 @@ def tile_extra_consensus_step_s13_kernel(
 
         def negate(on, c, g, lo, hi):
             i, at = piece_of[c]
-            src = prev_sb[i, g][:, :, at + lo : at + hi].rearrange("p t n -> p n t")
-            dst = neg[c, g][:, lo:hi, :]
+            src = prev_sb[i, g][:, :, at + lo : at + hi].rearrange("p t (n i) -> p n t i", i=4)
+            dst = neg[c, g][:, lo:hi, :].rearrange("p (n i) t -> p n t i", i=4)
             if on == "g":
                 nc.gpsimd.tensor_scalar(out=dst, in0=src, scalar1=-1.0, scalar2=0.0, op0=ALU.mult, op1=ALU.add)
             else:
@@ -227,11 +230,15 @@ def tile_extra_consensus_step_s13_kernel(
             if b == 0:
                 x1_grp[c, g] = flow.tile([P, WIDTHS[c], T], BF16, name="x1_grp", bufs=3, align_bytes=64)
             cols = slice(b * P, (b + 1) * P)
+            if (c, g) in DIRECT:
+                other, op = prev_sb[c, g][:, :, cols].rearrange("p t n -> p n t"), ALU.add
+            else:
+                other, op = neg[c, g][:, cols, :], ALU.subtract
             nc.vector.tensor_tensor(
                 out=x1_grp[c, g][:, cols, :],
                 in0=first[c, u][:].rearrange("p t n -> p n t"),
-                in1=neg[c, g][:, cols, :],
-                op=ALU.subtract,
+                in1=other,
+                op=op,
             )
 
         def quant_x1(c, g):
@@ -288,6 +295,9 @@ def tile_extra_consensus_step_s13_kernel(
                 nc.vector.tensor_tensor(out=res[:], in0=late[j][:], in1=step, op=ALU.subtract)
             nc.sync.dma_start(out=out[m * P : (m + 1) * P, cols], in_=res[:])
 
+        dummy = psum.tile([P, 512], F32, name="dummy", tag="first", bufs=EARLY)
+        for _ in range(5):
+            nc.tensor.matmul(dummy[:], warm_w[:, :P], warm_w[:], start=True, stop=True)
         vcopy, scopy = nc.vector.tensor_copy, nc.scalar.copy
         for t in range(T):
             widen("v", 0, t, 0, 256)
@@ -317,8 +327,8 @@ def tile_extra_consensus_step_s13_kernel(
             widen("s", 1, t, 0, 512)
         group_dict(1, 0, 256)
         group_dict(1, 256, 512)
-        for b in range(4):
-            negate("g", 1, 0, b * 128, (b + 1) * 128)
+        for h in range(2):
+            negate("s", 1, 0, h * 256, (h + 1) * 256)
         for h in range(2):
             negate("s", 1, 1, h * 256, (h + 1) * 256)
 

@@ -68,10 +68,10 @@ def tile_extra_consensus_step_s13_kernel(
         words = [sb("avg_w", [P, G, 2 * A], U8), sb("mix_w", [P, G, 2 * A], U8)]
         gst = [sb(f"gstep{i}", [P, 2, D], BF16) for i in range(M // 2)]
 
+        nc.vector.memset(planes[:].bitcast(I32), 0)
         warm_w = sb("warm_w", [P, 512], BF16)
         nc.vector.memset(warm_w[:], 0.0)
         nc.vector.memset(warm_in[:], 0.0)
-        nc.vector.memset(planes[:].bitcast(I32), 0)
         nc.scalar.activation(out=warm_out[:], in_=warm_in[:], func=COPY, scale=-1.0)
 
         load = nc.sync.dma_start
@@ -94,9 +94,9 @@ def tile_extra_consensus_step_s13_kernel(
         def load_gstep(i):
             load(out=gst[i][:], in_=gstep_v[:, 2 * i : 2 * i + 2, :])
 
-        def load_scales(which, s_hbm):
+        def load_scales(which, s_hbm, lo=0, hi=4):
             rows = s_hbm.bitcast(I32).rearrange("g (q i) n -> i q g n", i=4)
-            for i in range(4):
+            for i in range(lo, hi):
                 load(out=planes[i:P:32, G * which : G * which + G, :].bitcast(I32), in_=rows[i])
 
         def load_words(which, w_hbm):
@@ -106,14 +106,14 @@ def tile_extra_consensus_step_s13_kernel(
         load_dict(0)
         load_code(0, 0, 2)
         load_code(0, 2, 4)
+        load_scales(0, avg_scales, 0, 4)
         load_prev(0, 0)
         load_code(1)
         load_prev(0, 1)
         load_dict(1)
         load_words(0, avg_words)
-        load_scales(0, avg_scales)
-        load_scales(1, mix_scales)
         load_prev(1, 0)
+        load_scales(1, mix_scales, 0, 4)
         load_words(1, mix_words)
         load_prev(1, 1)
         load_gstep(0)
@@ -285,6 +285,18 @@ def tile_extra_consensus_step_s13_kernel(
             c, m = divmod(j, M)
             w = WIDTHS[c]
             cols = slice(STARTS[c], STARTS[c] + w)
+            if j == C * M - 1:
+                for lo in range(0, w, w // 2):
+                    part = flow.tile([P, w // 2], F32, name="part", bufs=2, align_bytes=64)
+                    at = STARTS[c] + lo
+                    nc.vector.tensor_tensor(
+                        out=part[:],
+                        in0=late[j][:, lo : lo + w // 2],
+                        in1=gst[m // 2][:, m % 2, at : at + w // 2],
+                        op=ALU.subtract,
+                    )
+                    nc.sync.dma_start(out=out[m * P : (m + 1) * P, at : at + w // 2], in_=part[:])
+                return
             res = flow.tile([P, w], F32, name="res", bufs=12, align_bytes=64)
             step = gst[m // 2][:, m % 2, cols]
             if j in GP_SUB:

@@ -28,7 +28,7 @@ PIECES = ((0,), (1,), (2,))
 AHEAD = 4
 LATE = 5
 EARLY = 8 - LATE
-DIRECT = ()
+DIRECT = ((0,0),)
 GP_SUB = (2,4,6,8)
 V_WIDEN = (0,)
 GROUPERS = ("v", "s", "s")
@@ -44,7 +44,7 @@ def tile_extra_consensus_step_s13_kernel(
         psum = ctx.enter_context(tc.psum_pool(name="psum", bufs=1))
 
         def sb(name, shape, dtype):
-            return keep.tile(shape, dtype, name=name, align_bytes=64)
+            return keep.tile(shape, dtype, name=name, align_bytes=256)
 
         ident = sb("ident", [P, P], F32)
         make_identity(nc, ident[:])
@@ -179,8 +179,8 @@ def tile_extra_consensus_step_s13_kernel(
             else:
                 nc.gpsimd.tensor_scalar(out=dst, in0=src, scalar1=1.0, scalar2=0.0, op0=ALU.mult, op1=ALU.add)
 
-        def quant_dict(c):
-            quant(dgrp[c][:].rearrange("p n t -> p (n t)"), dict_q[c][:], dict_s[c][:])
+        def quant_dict(c, lo=0, hi=512):
+            quant(dgrp[c][:, lo:hi, :].rearrange("p n t -> p (n t)"), dict_q[c][:, lo:hi], dict_s[c][:, lo:hi])
 
         neg = {(c, g): sb(f"neg{c}_{g}", [P, WIDTHS[c], T], BF16) for c in range(C) for g in range(G)}
         neg_q = {(c, g): sb(f"neg_q{c}_{g}", [P, WIDTHS[c]], U32) for c in range(C) for g in range(G)}
@@ -228,7 +228,7 @@ def tile_extra_consensus_step_s13_kernel(
         def add_prev(c, u):
             g, b = divmod(u, WIDTHS[c] // P)
             if b == 0:
-                x1_grp[c, g] = flow.tile([P, WIDTHS[c], T], BF16, name="x1_grp", bufs=3, align_bytes=64)
+                x1_grp[c, g] = flow.tile([P, WIDTHS[c], T], BF16, name="x1_grp", bufs=3, align_bytes=256)
             cols = slice(b * P, (b + 1) * P)
             if (c, g) in DIRECT:
                 other, op = prev_sb[c, g][:, :, cols].rearrange("p t n -> p n t"), ALU.add
@@ -287,7 +287,7 @@ def tile_extra_consensus_step_s13_kernel(
             cols = slice(STARTS[c], STARTS[c] + w)
             if j == C * M - 1:
                 for lo in range(0, w, w // 2):
-                    part = flow.tile([P, w // 2], F32, name="part", bufs=2, align_bytes=64)
+                    part = flow.tile([P, w // 2], F32, name="part", bufs=2, align_bytes=256)
                     at = STARTS[c] + lo
                     nc.vector.tensor_tensor(
                         out=part[:],
@@ -297,10 +297,10 @@ def tile_extra_consensus_step_s13_kernel(
                     )
                     nc.sync.dma_start(out=out[m * P : (m + 1) * P, at : at + w // 2], in_=part[:])
                 return
-            res = flow.tile([P, w], F32, name="res", bufs=12, align_bytes=64)
+            res = flow.tile([P, w], F32, name="res", bufs=12, align_bytes=256)
             step = gst[m // 2][:, m % 2, cols]
             if j in GP_SUB:
-                raw = flow.tile([P, w], F32, name="raw", bufs=3, align_bytes=64)
+                raw = flow.tile([P, w], F32, name="raw", bufs=3, align_bytes=256)
                 nc.scalar.copy(out=raw[:], in_=late[j][:])
                 nc.gpsimd.tensor_tensor(out=res[:], in0=raw[:], in1=step, op=ALU.subtract)
             else:
@@ -321,18 +321,19 @@ def tile_extra_consensus_step_s13_kernel(
         turn(0, 1)
         untangle(scopy, 0, 0)
         untangle(scopy, 0, 1)
-        quant_dict(0)
+        quant_dict(0, 0, 256)
         quant_code(0)
+        quant_dict(0, 256, 512)
         stage1(0, 0)
         stage1(0, 1)
         turn(1, 0)
         turn(1, 1)
         negate("s", 0, 0, 0, 128)
         negate("s", 0, 0, 128, 256)
-        negate("g", 0, 0, 256, 384)
-        negate("g", 0, 0, 384, 512)
         untangle(scopy, 1, 0)
         untangle(scopy, 1, 1)
+        negate("s", 0, 0, 256, 384)
+        negate("s", 0, 0, 384, 512)
         for b in range(4):
             negate("g", 0, 1, b * 128, (b + 1) * 128)
         for t in range(T):

from contextlib import ExitStack

import concourse.mybir as mybir
from concourse.masks import make_identity

A, K, D = 1024, 512, 1536
FLOPS = 2 * A * K * D + 2 * (2 * A * A * D)

F32 = mybir.dt.float32
BF16 = mybir.dt.bfloat16
I32 = mybir.dt.int32
U32 = mybir.dt.uint32
U8 = mybir.dt.uint8
FP8 = mybir.dt.float8_e4m3fn
FP8X4 = mybir.dt.float8_e4m3fn_x4
FP4X4 = mybir.dt.float4_e2m1fn_x4
ALU = mybir.AluOpType
COPY = mybir.ActivationFunctionType.Copy

P = 128
T = 4
G = A // 512
M = A // P
WIDTHS = (512, 512, 512)
STARTS = tuple(sum(WIDTHS[:c]) for c in range(len(WIDTHS)))
C = len(WIDTHS)
PIECES = ((0,), (1,), (2,))
AHEAD = 4
LATE = 5
EARLY = 8 - LATE
DIRECT = ((0,0),)
GP_SUB = (2,4,6,8)
V_WIDEN = (0,)
GROUPERS = ("v", "s", "s")


def tile_extra_consensus_step_s13_kernel(
    tc, code, dictionary_bytes, dictionary_scale, prev, gstep, mix_words, mix_scales, avg_words, avg_scales, out
):
    nc = tc.nc
    with ExitStack() as ctx:
        keep = ctx.enter_context(tc.tile_pool(name="keep", bufs=1))
        flow = ctx.enter_context(tc.tile_pool(name="flow", bufs=8))
        psum = ctx.enter_context(tc.psum_pool(name="psum", bufs=1))

        def sb(name, shape, dtype):
            return keep.tile(shape, dtype, name=name, align_bytes=256)

        ident = sb("ident", [P, P], F32)
        make_identity(nc, ident[:])
        planes = sb("planes", [P, 2 * G, A], U8)
        warm_in = sb("warm_in", [P, 16], F32)
        warm_out = sb("warm_out", [P, 16], F32)

        ctx.enter_context(tc.manual_schedule())

        dscale = sb("dscale", [P, T], F32)
        code_sb = [sb(f"code{g}", [P, T, K], BF16) for g in range(G)]
        dbytes, prev_sb = {}, {}
        piece_cols = []
        for i, chunks in enumerate(PIECES):
            lo = STARTS[chunks[0]]
            hi = STARTS[chunks[-1]] + WIDTHS[chunks[-1]]
            piece_cols.append((lo, hi))
            dbytes[i] = sb(f"dbytes{i}", [P, T, hi - lo], U8)
            for g in range(G):
                prev_sb[i, g] = sb(f"prev{i}_{g}", [P, T, hi - lo], BF16)
        words = [sb("avg_w", [P, G, 2 * A], U8), sb("mix_w", [P, G, 2 * A], U8)]
        gst = [sb(f"gstep{i}", [P, 2, D], BF16) for i in range(M // 2)]

        nc.vector.memset(planes[:].bitcast(I32), 0)
        warm_w = sb("warm_w", [P, 512], BF16)
        nc.vector.memset(warm_w[:], 0.0)
        nc.vector.memset(warm_in[:], 0.0)
        nc.scalar.activation(out=warm_out[:], in_=warm_in[:], func=COPY, scale=-1.0)

        load = nc.sync.dma_start
        dict_v = dictionary_bytes.rearrange("(p t) n -> p t n", t=T)
        code_v = code.rearrange("(g m t) k -> g m t k", m=P, t=T)
        prev_v = prev.rearrange("(g p t) d -> g p t d", p=P, t=T)
        gstep_v = gstep.rearrange("(m p) d -> p m d", p=P)

        def load_code(g, lo=0, hi=T):
            load(out=code_sb[g][:, lo:hi], in_=code_v[g][:, lo:hi])

        def load_prev(i, g):
            lo, hi = piece_cols[i]
            load(out=prev_sb[i, g][:], in_=prev_v[g][:, :, lo:hi])

        def load_dict(i):
            lo, hi = piece_cols[i]
            load(out=dbytes[i][:], in_=dict_v[:, :, lo:hi])

        def load_gstep(i):
            load(out=gst[i][:], in_=gstep_v[:, 2 * i : 2 * i + 2, :])

        def load_scales(which, s_hbm, lo=0, hi=4):
            rows = s_hbm.bitcast(I32).rearrange("g (q i) n -> i q g n", i=4)
            for i in range(lo, hi):
                load(out=planes[i:P:32, G * which : G * which + G, :].bitcast(I32), in_=rows[i])

        def load_words(which, w_hbm):
            load(out=words[which][:].bitcast(I32), in_=w_hbm.rearrange("g p b -> p g b").bitcast(I32))

        load(out=dscale[:], in_=dictionary_scale.rearrange("(p t) o -> p (t o)", t=T))
        load_dict(0)
        load_code(0, 0, 2)
        load_code(0, 2, 4)
        load_scales(0, avg_scales, 0, 4)
        load_prev(0, 0)
        load_code(1)
        load_prev(0, 1)
        load_dict(1)
        load_words(0, avg_words)
        load_prev(1, 0)
        load_scales(1, mix_scales, 0, 4)
        load_words(1, mix_words)
        load_prev(1, 1)
        load_gstep(0)
        load_dict(2)
        load_gstep(1)
        load_gstep(2)
        load_prev(2, 0)
        load_gstep(3)
        load_prev(2, 1)

        code_grp = [sb(f"code_grp{g}", [P, T, P, T], BF16) for g in range(G)]
        code_q = [sb(f"code_q{g}", [P, T * P], U32) for g in range(G)]
        code_s = [sb(f"code_s{g}", [P, T * P], U8) for g in range(G)]
        turned = {}

        def turn(g, h):
            bank = psum.tile([P, 2, 2, P], F32, name="turn", tag="late", bufs=LATE)
            for j in range(2):
                w = code_sb[g][:, 2 * h + j, :].bitcast(F32)
                for u in range(2):
                    nc.tensor.transpose(bank[:, j, u, :], w[:, u : K // 2 : 2], ident[:])
            turned[g, h] = bank

        def untangle(copy, g, h):
            dst = code_grp[g][:, 2 * h : 2 * h + 2].rearrange("p j m t -> p j (m t)").bitcast(F32)
            copy(
                out=dst.rearrange("p j (m u) -> p j m u", u=2),
                in_=turned[g, h][:].rearrange("p j u m -> p j m u"),
            )

        def quant(src, codes, scales):
            nc.vector.quantize_mx(out=codes.bitcast(FP8X4), scales=scales, in_=src)

        def quant_code(g):
            quant(code_grp[g][:].rearrange("p a m t -> p (a m t)"), code_q[g][:], code_s[g][:])

        piece_of = {}
        for i, chunks in enumerate(PIECES):
            for c in chunks:
                piece_of[c] = i, STARTS[c] - piece_cols[i][0]

        dwide = [sb(f"dwide{c}", [P, T, WIDTHS[c]], BF16) for c in range(C)]
        dgrp = [sb(f"dgrp{c}", [P, WIDTHS[c], T], BF16) for c in range(C)]
        dict_q = [sb(f"dict_q{c}", [P, WIDTHS[c]], U32) for c in range(C)]
        dict_s = [sb(f"dict_s{c}", [P, WIDTHS[c]], U8) for c in range(C)]

        def widen(on, c, t, lo, hi):
            src = dbytes[c][:, t, lo:hi].bitcast(FP8)
            dst = dwide[c][:, t, lo:hi]
            factor = dscale[:, t : t + 1]
            if on == "v":
                nc.vector.tensor_scalar(out=dst, in0=src, scalar1=factor, scalar2=None, op0=ALU.mult)
            else:
                nc.scalar.activation(out=dst, in_=src, func=COPY, scale=factor)

        def group_dict(c, lo, hi):
            src = dwide[c][:, :, lo:hi].rearrange("p t (n i) -> p n t i", i=4)
            dst = dgrp[c][:, lo:hi, :].rearrange("p (n i) t -> p n t i", i=4)
            if GROUPERS[c] == "v":
                nc.vector.tensor_copy(out=dst, in_=src)
            elif GROUPERS[c] == "s":
                nc.scalar.copy(out=dst, in_=src)
            else:
                nc.gpsimd.tensor_scalar(out=dst, in0=src, scalar1=1.0, scalar2=0.0, op0=ALU.mult, op1=ALU.add)

        def quant_dict(c, lo=0, hi=512):
            quant(dgrp[c][:, lo:hi, :].rearrange("p n t -> p (n t)"), dict_q[c][:, lo:hi], dict_s[c][:, lo:hi])

        neg = {(c, g): sb(f"neg{c}_{g}", [P, WIDTHS[c], T], BF16) for c in range(C) for g in range(G)}
        neg_q = {(c, g): sb(f"neg_q{c}_{g}", [P, WIDTHS[c]], U32) for c in range(C) for g in range(G)}
        neg_s = {(c, g): sb(f"neg_s{c}_{g}", [P, WIDTHS[c]], U8) for c in range(C) for g in range(G)}

        def negate(on, c, g, lo, hi):
            i, at = piece_of[c]
            src = prev_sb[i, g][:, :, at + lo : at + hi].rearrange("p t (n i) -> p n t i", i=4)
            dst = neg[c, g][:, lo:hi, :].rearrange("p (n i) t -> p n t i", i=4)
            if on == "g":
                nc.gpsimd.tensor_scalar(out=dst, in0=src, scalar1=-1.0, scalar2=0.0, op0=ALU.mult, op1=ALU.add)
            else:
                nc.scalar.activation(out=dst, in_=src, func=COPY, scale=-1.0)

        def quant_neg(c, g):
            quant(neg[c, g][:].rearrange("p n t -> p (n t)"), neg_q[c, g][:], neg_s[c, g][:])

        x1_q = {(c, g): sb(f"x1_q{c}_{g}", [P, WIDTHS[c]], U32) for c in range(C) for g in range(G)}
        x1_s = {(c, g): sb(f"x1_s{c}_{g}", [P, WIDTHS[c]], U8) for c in range(C) for g in range(G)}
        x1_grp = {}
        first = {}

        def units(c):
            return G * WIDTHS[c] // P

        def stage1(c, u):
            if u >= units(c):
                return
            g, b = divmod(u, WIDTHS[c] // P)
            cols = slice(b * P, (b + 1) * P)
            bank = psum.tile([P, T, P], F32, name="first", tag="first", bufs=EARLY)
            for t in range(T):
                rows = slice(t * P, (t + 1) * P)
                nc.tensor.matmul_mx(
                    out=bank[:, t, :],
                    lhsT=code_q[g][:, rows].bitcast(FP8X4),
                    lhsT_scale=code_s[g][:, rows],
                    rhs=dict_q[c][:, cols].bitcast(FP8X4),
                    rhs_scale=dict_s[c][:, cols],
                    start=True,
                    stop=True,
                )
            first[c, u] = bank

        def add_prev(c, u):
            g, b = divmod(u, WIDTHS[c] // P)
            if b == 0:
                x1_grp[c, g] = flow.tile([P, WIDTHS[c], T], BF16, name="x1_grp", bufs=3, align_bytes=256)
            cols = slice(b * P, (b + 1) * P)
            if (c, g) in DIRECT:
                other, op = prev_sb[c, g][:, :, cols].rearrange("p t n -> p n t"), ALU.add
            else:
                other, op = neg[c, g][:, cols, :], ALU.subtract
            nc.vector.tensor_tensor(
                out=x1_grp[c, g][:, cols, :],
                in0=first[c, u][:].rearrange("p t n -> p n t"),
                in1=other,
                op=op,
            )

        def quant_x1(c, g):
            quant(x1_grp[c, g][:].rearrange("p n t -> p (n t)"), x1_q[c, g][:], x1_s[c, g][:])

        late = {}
        started = {}

        def mix_pass(j, b, k):
            c, m = divmod(j, M)
            which, g = divmod(k, G)
            wide = WIDTHS[c] == 512
            cols = slice(0, 512) if wide else slice(b * P, (b + 1) * P)
            codes, scales = ((neg_q, neg_s), (x1_q, x1_s))[which]
            nc.tensor.matmul_mx(
                out=late[j][:, cols],
                lhsT=words[which][:, g, 2 * P * m : 2 * P * (m + 1)].bitcast(FP4X4),
                lhsT_scale=planes[:, G * which + g, P * m : P * (m + 1)],
                rhs=codes[c, g][:, cols].bitcast(FP8X4),
                rhs_scale=scales[c, g][:, cols],
                start=k == 0,
                stop=k == 2 * G - 1,
            )

        def advance(j, upto):
            if j >= C * M:
                return
            if j not in late:
                tag, bufs = ("late", LATE) if j < C * M - EARLY else ("first", EARLY)
                late[j] = psum.tile([P, WIDTHS[j // M]], F32, name="late", tag=tag, bufs=bufs)
                started[j] = 0
            for k in range(started[j], upto):
                mix_pass(j, 0, k)
            started[j] = max(upto, started[j])

        def mix(j):
            advance(j, 2 * G)
            if WIDTHS[j // M] < 512:
                for b in range(1, WIDTHS[j // M] // P):
                    for k in range(2 * G):
                        mix_pass(j, b, k)

        def finish(j):
            c, m = divmod(j, M)
            w = WIDTHS[c]
            cols = slice(STARTS[c], STARTS[c] + w)
            if j == C * M - 1:
                for lo in range(0, w, w // 2):
                    part = flow.tile([P, w // 2], F32, name="part", bufs=2, align_bytes=256)
                    at = STARTS[c] + lo
                    nc.vector.tensor_tensor(
                        out=part[:],
                        in0=late[j][:, lo : lo + w // 2],
                        in1=gst[m // 2][:, m % 2, at : at + w // 2],
                        op=ALU.subtract,
                    )
                    nc.sync.dma_start(out=out[m * P : (m + 1) * P, at : at + w // 2], in_=part[:])
                return
            res = flow.tile([P, w], F32, name="res", bufs=12, align_bytes=256)
            step = gst[m // 2][:, m % 2, cols]
            if j in GP_SUB:
                raw = flow.tile([P, w], F32, name="raw", bufs=3, align_bytes=256)
                nc.scalar.copy(out=raw[:], in_=late[j][:])
                nc.gpsimd.tensor_tensor(out=res[:], in0=raw[:], in1=step, op=ALU.subtract)
            else:
                nc.vector.tensor_tensor(out=res[:], in0=late[j][:], in1=step, op=ALU.subtract)
            nc.sync.dma_start(out=out[m * P : (m + 1) * P, cols], in_=res[:])

        dummy = psum.tile([P, 512], F32, name="dummy", tag="first", bufs=EARLY)
        for _ in range(5):
            nc.tensor.matmul(dummy[:], warm_w[:, :P], warm_w[:], start=True, stop=True)
        vcopy, scopy = nc.vector.tensor_copy, nc.scalar.copy
        for t in range(T):
            widen("v", 0, t, 0, 256)
        for t in range(T):
            widen("s", 0, t, 256, 512)
        group_dict(0, 0, 256)
        group_dict(0, 256, 512)
        turn(0, 0)
        turn(0, 1)
        untangle(scopy, 0, 0)
        untangle(scopy, 0, 1)
        quant_dict(0, 0, 256)
        quant_code(0)
        quant_dict(0, 256, 512)
        stage1(0, 0)
        stage1(0, 1)
        turn(1, 0)
        turn(1, 1)
        negate("s", 0, 0, 0, 128)
        negate("s", 0, 0, 128, 256)
        untangle(scopy, 1, 0)
        untangle(scopy, 1, 1)
        negate("s", 0, 0, 256, 384)
        negate("s", 0, 0, 384, 512)
        for b in range(4):
            negate("g", 0, 1, b * 128, (b + 1) * 128)
        for t in range(T):
            widen("s", 1, t, 0, 512)
        group_dict(1, 0, 256)
        group_dict(1, 256, 512)
        for h in range(2):
            negate("s", 1, 0, h * 256, (h + 1) * 256)
        for h in range(2):
            negate("s", 1, 1, h * 256, (h + 1) * 256)

        for u in range(8):
            if u == 3:
                quant_code(1)
                stage1(0, 4)
            if u != 2:
                stage1(0, u + 2)
            add_prev(0, u)
            if u == 3:
                quant_neg(0, 0)
                for j in range(LATE):
                    advance(j, 1)
            if u == 4:
                quant_x1(0, 0)
            if u == 5:
                quant_neg(0, 1)
                for j in range(LATE):
                    advance(j, 2)
        quant_dict(1)
        stage1(1, 0)
        stage1(1, 1)
        for j in range(LATE):
            advance(j, 3)
        quant_x1(0, 1)

        side = {
            0: [lambda t=t: widen("s", 2, t, 0, 512) for t in range(T)]
            + [lambda h=h: group_dict(2, h * 256, (h + 1) * 256) for h in range(2)]
            + [lambda h=h: negate("s", 2, 0, h * 256, (h + 1) * 256) for h in range(2)],
            1: [lambda h=h: negate("s", 2, 1, h * 256, (h + 1) * 256) for h in range(2)],
        }
        for c in range(C):
            more = c + 1 < C
            todo = side.get(c, [])
            if c == 0:
                mix(0)
            if more and c > 0:
                stage1(c + 1, 0)
                stage1(c + 1, 1)
            for i in range(M):
                j = c * M + i
                for task in todo[:1]:
                    task()
                todo = todo[1:]
                if j > 0:
                    mix(j)
                if more:
                    stage1(c + 1, i + 2)
                    add_prev(c + 1, i)
                    if i == 1:
                        quant_neg(c + 1, 0)
                    if i == 3:
                        quant_neg(c + 1, 1)
                    if i == 4:
                        quant_x1(c + 1, 0)
                if j + AHEAD < C * M - EARLY:
                    advance(j + AHEAD, 2)
                if c == C - 1 and i in (2, 4):
                    advance(C * M - EARLY + i // 2, 3)
                if more and i >= 5:
                    advance((c + 1) * M + i - 5, 3)
                finish(j)
                if c + 2 < C and i == 6:
                    quant_dict(c + 2)
            if more:
                quant_x1(c + 1, 1)
            advance((c + 1) * M + 3, 3)
            if c == C - 2:
                advance(C * M - EARLY, 3)
